import numpy as np
import ml_dtypes


def mxq(x, axis, fmt="e4m3"):
    dtype, down = {"e4m3": (ml_dtypes.float8_e4m3fn, 7), "e5m2": (ml_dtypes.float8_e5m2, 14)}[fmt]
    v = np.moveaxis(np.asarray(x, np.float32).astype(ml_dtypes.bfloat16).astype(np.float64), axis, -1)
    blocks = v.reshape(v.shape[:-1] + (-1, 32))
    amax = np.abs(blocks).max(-1, keepdims=True)
    byte = np.maximum(np.where(amax > 0, np.frexp(amax)[1] - 1 + 127, 0) - down, 1)
    scale = np.exp2(byte - 127.0)
    codes = (blocks / scale).astype(np.float32).astype(dtype).astype(np.float64)
    return np.moveaxis((codes * scale).reshape(v.shape), -1, axis)


WIDE = False


def mx_kscale(k):
    if not WIDE:
        return np.ones(k)
    levels = np.array([10, -10, 5, -5, 0])
    if k % 512:
        return np.exp2(np.random.permutation(np.resize(levels, k // 32))).repeat(32)
    a = np.empty((k // 512, 16))
    for p in range(k // 512):
        a[p, :8] = np.random.permutation(np.resize(levels, 8))
        for g in range(8):
            far = levels[np.abs(levels - a[p, g]) >= 10]
            a[p, g + 8] = far[np.random.randint(len(far))]
    return np.exp2(a.ravel()).repeat(32)


def f64(x):
    return np.asarray(x).astype(np.float64)


def striped(idx):
    return np.tile(idx.reshape(-1, 16).T, (8, 1)).astype(np.uint16)


def unstriped(offs):
    return offs[:16].T.reshape(-1).astype(np.int64)


def striped8(idx):
    return np.concatenate([x.reshape(-1, 16).T for x in idx]).astype(np.uint16)


def runs(offs, k):
    lists = np.stack([offs[16 * r : 16 * r + 16].T.reshape(-1) for r in range(8)]).astype(np.int64)
    return lists[np.arange(k) % 512 // 64]


def pack_weight(w):
    k, n = w.shape
    w = f64(np.asarray(w, np.float32).astype(ml_dtypes.bfloat16)).reshape(k // 32, 32, n)
    amax = np.abs(w).max(1)
    byte = np.clip(np.where(amax > 0, np.frexp(amax)[1] - 1 + 127 - 7, 1), 1, 254)
    scaled = (w * np.exp2(127.0 - byte)[:, None, :]).reshape(k, n).astype(np.float32)
    words = np.ascontiguousarray(scaled.reshape(k // 512, 128, 4, n).transpose(0, 1, 3, 2)).astype(ml_dtypes.float8_e4m3fn).view(np.uint8)
    return words, np.ascontiguousarray(byte.astype(np.uint8).reshape(k // 512, 16, n))


def unpack_weight(words, scales):
    g, p, n, _ = words.shape
    vals = np.ascontiguousarray(words).view(ml_dtypes.float8_e4m3fn).astype(np.float64) * np.repeat(np.exp2(scales.astype(np.float64) - 127.0), 8, axis=1)[..., None]
    return vals.transpose(0, 1, 3, 2).reshape(g * 512, n)


E2M1 = np.array([0.0, 0.5, 1.0, 1.5, 2.0, 3.0, 4.0, 6.0, -0.0, -0.5, -1.0, -1.5, -2.0, -3.0, -4.0, -6.0])


def pack_fp4(w):
    k, n = w.shape
    w = f64(np.asarray(w, np.float32).astype(ml_dtypes.bfloat16)).reshape(k // 32, 32, n)
    amax = np.abs(w).max(1)
    mant, ex = np.frexp(amax / 6.0)
    byte = np.clip(np.where(amax > 0, np.where(mant > 0.5, ex, ex - 1) + 127, 1), 1, 254)
    scaled = (w * np.exp2(127.0 - byte)[:, None, :]).reshape(k, n).astype(np.float32)
    c = np.ascontiguousarray(scaled.reshape(k // 512, 128, 4, n).transpose(0, 1, 3, 2)).astype(ml_dtypes.float4_e2m1fn).view(np.uint8) & 0xF
    words = (c[..., 0::2] | (c[..., 1::2] << 4)).reshape(k // 512, 128, 2 * n)
    return np.ascontiguousarray(words), np.ascontiguousarray(byte.astype(np.uint8).reshape(k // 512, 16, n))


def unpack_fp4(words, scales):
    g, _, n = scales.shape
    words = np.ascontiguousarray(words).reshape(g, 128, n, 2)
    nib = np.empty((g, 128, n, 4), np.uint8)
    nib[..., 0::2] = words & 0xF
    nib[..., 1::2] = words >> 4
    vals = E2M1[nib] * np.repeat(np.exp2(scales.astype(np.float64) - 127.0), 8, axis=1)[..., None]
    return vals.transpose(0, 1, 3, 2).reshape(g * 512, n)


def planes(y):
    n, m = y.shape
    v = y.astype(np.float32).astype(ml_dtypes.bfloat16).astype(np.float64).reshape(n // 32, 32, m)
    top = np.abs(v).max(1)
    byte = np.clip(np.where(top > 0, np.frexp(top)[1] - 1 + 127 - 7, 1), 1, 254)
    codes = (v * np.exp2(127.0 - byte)[:, None, :]).reshape(n, m).astype(np.float32).astype(ml_dtypes.float8_e4m3fn).view(np.uint8)
    words = codes.reshape(n // 512, 128, 4, m).transpose(0, 1, 3, 2)
    return np.ascontiguousarray(words), np.ascontiguousarray(byte.astype(np.uint8).reshape(n // 512, 16, m))


K, T, S, N, H, W = 512, 2048, 512, 512, 512, 384


def setup_inputs():
    n = np.random.standard_normal
    s = mx_kscale(K)[:, None]
    u = mx_kscale(H)
    packed_xT = pack_weight(n((K, T)) * s)
    packed_w1 = pack_fp4(n((K, H)) / np.sqrt(K) / s)
    packed_w2 = pack_fp4(n((H, N)) / np.sqrt(2 * H) / u[:, None])
    packed_w3 = pack_fp4(n((K, N)) / np.sqrt(2 * K) / s)
    return {
        "x_words": packed_xT[0],
        "x_scales": packed_xT[1],
        "w1_words": packed_w1[0],
        "w1_scales": packed_w1[1],
        "gn": (np.random.uniform(0.5, 1.5, (H, 1)) * u[:, None]).astype(np.float32),
        "w2_words": packed_w2[0],
        "w2_scales": packed_w2[1],
        "w3_words": packed_w3[0],
        "w3_scales": packed_w3[1],
        "offs": striped8(np.random.randint(0, T, (8, S))),
        "n1": striped(np.random.permutation(S)[:W]),
        "n2": striped(np.random.permutation(S)[:W]),
        "two": striped(np.random.permutation(T)[:S]),
        "n3": striped8(np.stack([np.random.permutation(S) for _ in range(8)])),
        "n4": striped8(np.stack([np.random.permutation(S) for _ in range(8)])),
    }


def reference(x_words, x_scales, w1_words, w1_scales, gn, w2_words, w2_scales, w3_words, w3_scales, offs, n1, n2, two, n3, n4):
    xq = unpack_weight(x_words, x_scales)[np.arange(K)[:, None], runs(offs, K)]
    y = unpack_fp4(w1_words, w1_scales).T @ xq
    old = y[:, unstriped(n1)]
    pa = y[:, unstriped(n2)]
    ra = old - np.tanh(pa)
    ds = y.copy()
    ds[:, unstriped(n1)] = ra
    z = f64(gn) * ds
    x_two = unpack_weight(x_words, x_scales)[:, unstriped(two)]
    h = unpack_fp4(w2_words, w2_scales).T @ mxq(z, 0, "e4m3") + unpack_fp4(w3_words, w3_scales).T @ x_two
    ex = np.exp(0.5 * h)
    out_0 = (2.0 * ex) / (ex + ex[np.arange(N)[:, None], runs(n3, N)] + ex[np.arange(N)[:, None], runs(n4, N)])
    return (out_0,) + planes(out_0)

@@ -1,0 +1,251 @@
+from contextlib import ExitStack
+
+import concourse.mybir as mybir
+
+K, T, S, N, H, W = 512, 2048, 512, 512, 512, 384
+FLOPS = 2 * S * (K * H + H * N + K * N)
+
+F32 = mybir.dt.float32
+BF16 = mybir.dt.bfloat16
+I32 = mybir.dt.int32
+U32 = mybir.dt.uint32
+U16 = mybir.dt.uint16
+U8 = mybir.dt.uint8
+FP8X4 = mybir.dt.float8_e4m3fn_x4
+FP4X4 = mybir.dt.float4_e2m1fn_x4
+ACT = mybir.ActivationFunctionType
+ALU = mybir.AluOpType
+
+P = 128
+PACK = 4
+WINDOW = 2 * W
+HALF = S // 2
+CHUNKS = ((0, 256, "vector", "scalar"), (256, 128, "scalar", "vector"), (384, 128, "scalar", "scalar"))
+
+
+def tile_picked_hmixktanhshare_none_po_kernel(
+    tc, x_words, x_scales, w1_words, w1_scales, gn, w2_words, w2_scales, w3_words, w3_scales,
+    offs, n1, n2, two, n3, n4, out_0, out_1, out_2,
+):
+    nc = tc.nc
+    with ExitStack() as ctx:
+        lists = ctx.enter_context(tc.tile_pool(name="lists", bufs=1))
+        sb = ctx.enter_context(tc.tile_pool(name="sb", bufs=1))
+        psum = ctx.enter_context(tc.psum_pool(name="psum", bufs=1))
+
+        def tile(name, shape, dtype):
+            return sb.tile(shape, dtype, name=name, align_bytes=64)
+
+        def load_list(name, src):
+            held = lists.tile(list(src.shape), U16, name=name)
+            nc.sync.dma_start(held[:], src)
+            return held
+
+        def load_scale_rows(queue, dst, src):
+            queue.dma_start(out=dst.bitcast(I32), in_=src[0].bitcast(I32))
+
+        def move_scale_rows(queue, dst, src):
+            for r in range(1, 4):
+                queue.dma_start(out=dst[r:P:32, :].bitcast(I32), in_=src[8 * r : P : 32, :].bitcast(I32))
+
+        def deal_words(name, raw):
+            dealt = tile(name, [P, 2 * N], U8)
+            nc.scalar.copy(
+                out=dealt[:].bitcast(U16).rearrange("p (t m) -> p t m", t=PACK),
+                in_=raw[:].bitcast(U16).rearrange("p (m t) -> p t m", t=PACK),
+            )
+            return dealt
+
+        def deal_scales(name, raw, count):
+            dealt = tile(name, [P, count * N], U8)
+            nc.vector.tensor_copy(
+                out=dealt[:].rearrange("p (w t m) -> p w t m", w=count, t=PACK),
+                in_=raw[:].rearrange("p (w m t) -> p w t m", w=count, t=PACK),
+            )
+            return dealt
+
+        def pick_scales(name, offsets, queue):
+            picked = tile(name + "_picked", [P, S], U8)
+            nc.vector.tensor_copy(picked[:], xs_table[:].indirect(offsets))
+            plane = tile(name, [P, S], U8)
+            nc.vector.tensor_copy(plane[:].bitcast(I32), picked[:].bitcast(I32))
+            move_scale_rows(queue, plane, picked)
+            return plane
+
+        xs_table = tile("xs_table", [P, T], U8)
+        nc.gpsimd.memset(xs_table[:].bitcast(I32), 0)
+        w1s_raw = tile("w1s_raw", [P, H], U8)
+        nc.vector.memset(w1s_raw[:].bitcast(I32), 0)
+        w23s_raw = tile("w23s_raw", [P, 2 * N], U8)
+        nc.vector.memset(w23s_raw[:].bitcast(I32), 0)
+        half_ds = [tile("half_ds%d" % t, [P, WINDOW], F32) for t in range(PACK)]
+        for t in range(PACK):
+            nc.vector.memset(half_ds[t][:, S:WINDOW], 0.0)
+        minus_half = tile("minus_half", [P, W], F32)
+        nc.vector.memset(minus_half[:], -0.5)
+
+        xw_table = tile("xw_table", [P, T], U32)
+        nc.scalar.dma_start(out=xw_table[:].bitcast(I32), in_=x_words[0].rearrange("p n t -> p (n t)").bitcast(I32))
+        offs_t = load_list("offs_t", offs)
+        load_scale_rows(nc.sync, xs_table[0:P:8, :], x_scales)
+        two_t = load_list("two_t", two)
+        n2_t = load_list("n2_t", n2)
+        n1_t = load_list("n1_t", n1)
+        n3_t = load_list("n3_t", n3)
+        n4_t = load_list("n4_t", n4)
+
+        load_scale_rows(nc.gpsimd, w1s_raw[0:P:8, :], w1_scales)
+        w1w_raw = tile("w1w_raw", [P, 2 * H], U8)
+        nc.gpsimd.dma_start(out=w1w_raw[:].bitcast(I32), in_=w1_words[0].bitcast(I32))
+        w3w_raw = tile("w3w_raw", [P, 2 * N], U8)
+        nc.gpsimd.dma_start(out=w3w_raw[:].bitcast(I32), in_=w3_words[0].bitcast(I32))
+        w2w_raw = tile("w2w_raw", [P, 2 * N], U8)
+        nc.gpsimd.dma_start(out=w2w_raw[:].bitcast(I32), in_=w2_words[0].bitcast(I32))
+        load_scale_rows(nc.gpsimd, w23s_raw[0:P:8, 0:N], w2_scales)
+        load_scale_rows(nc.gpsimd, w23s_raw[0:P:8, N : 2 * N], w3_scales)
+        gain = tile("gain", [P, PACK], F32)
+        nc.gpsimd.dma_start(out=gain[:], in_=gn.rearrange("(p t) o -> p (t o)", t=PACK))
+
+        xs_offs = pick_scales("xs_offs", offs_t[:], nc.scalar)
+        w1s = deal_scales("w1s", w1s_raw, 1)
+        move_scale_rows(nc.sync, w1s, w1s)
+        w1w = deal_words("w1w", w1w_raw)
+        xw_offs = tile("xw_offs", [P, S], U32)
+        nc.vector.tensor_copy(xw_offs[:], xw_table[:].indirect(offs_t[:]))
+        xs_two = pick_scales("xs_two", two_t[:], nc.sync)
+        xw_two = tile("xw_two", [P, S], U32)
+        nc.vector.tensor_copy(xw_two[:], xw_table[:].indirect(two_t[:]))
+        w3w = deal_words("w3w", w3w_raw)
+        w2w = deal_words("w2w", w2w_raw)
+        w23s = deal_scales("w23s", w23s_raw, 2)
+        move_scale_rows(nc.sync, w23s, w23s)
+        w2s = w23s[:, 0:N]
+        w3s = w23s[:, N : 2 * N]
+
+        def product(bank, words, scales, t, rhs, rhs_scale, start, stop):
+            nc.tensor.matmul_mx(
+                out=bank,
+                lhsT=words[:, 2 * P * t : 2 * P * (t + 1)].bitcast(FP4X4),
+                lhsT_scale=scales[:, P * t : P * (t + 1)],
+                rhs=rhs.bitcast(FP8X4),
+                rhs_scale=rhs_scale,
+                start=start,
+                stop=stop,
+            )
+
+        y_bank = [psum.tile([P, S], F32, name="y_bank%d" % t) for t in range(PACK)]
+        h_bank = [psum.tile([P, S], F32, name="h_bank%d" % t) for t in range(PACK)]
+        for t in range(PACK):
+            product(y_bank[t][:], w1w, w1s, t, xw_offs[:], xs_offs[:], True, True)
+
+        for t in range(PACK):
+            product(h_bank[t][:], w3w, w3s, t, xw_two[:], xs_two[:], True, False)
+
+        sig = [tile("sig%d" % t, [P, W], F32) for t in range(PACK)]
+        summed = [tile("summed%d" % t, [P, W], F32) for t in range(PACK)]
+        z_rows = tile("z_rows", [P, PACK, S], BF16)
+        gain2 = tile("gain2", [P, PACK], F32)
+        nc.vector.tensor_scalar(gain2[:], gain[:], 2.0, None, ALU.mult)
+
+        def evac(engine, t):
+            if engine == "vector":
+                nc.vector.tensor_scalar(half_ds[t][:, 0:S], y_bank[t][:], 0.5, None, ALU.mult)
+            else:
+                nc.scalar.activation(half_ds[t][:, 0:S], y_bank[t][:], ACT.Copy, scale=0.5)
+
+        def gather(engine, dst, window, offsets):
+            if engine == "vector":
+                nc.vector.tensor_copy(dst, window.indirect(offsets))
+            else:
+                nc.scalar.activation(dst, window.indirect(offsets), ACT.Copy)
+
+        def sigmoid_of_pa(t):
+            nc.scalar.activation(sig[t][:], half_ds[t][:].indirect(n2_t[:]), ACT.Sigmoid, scale=-4.0)
+
+        def add_old(t):
+            nc.vector.tensor_tensor(summed[t][:], half_ds[t][:].indirect(n1_t[:]), sig[t][:], ALU.add)
+
+        def scatter(engine, t):
+            if engine == "vector":
+                nc.vector.tensor_tensor(half_ds[t][:].indirect(n1_t[:]), summed[t][:], minus_half[:], ALU.add)
+            else:
+                nc.scalar.activation(half_ds[t][:].indirect(n1_t[:]), summed[t][:], ACT.Copy, bias=-0.5)
+
+        def gain_round(engine, t):
+            if engine == "vector":
+                nc.vector.tensor_scalar(z_rows[:, t, :], half_ds[t][:, 0:S], gain2[:, t : t + 1], None, ALU.mult)
+            else:
+                nc.scalar.activation(z_rows[:, t, :], half_ds[t][:, 0:S], ACT.Copy, scale=gain2[:, t : t + 1])
+
+        evac("vector", 0)
+        sigmoid_of_pa(0)
+        evac("vector", 1)
+        sigmoid_of_pa(1)
+        add_old(0)
+        evac("vector", 2)
+        sigmoid_of_pa(2)
+        add_old(1)
+        scatter("scalar", 0)
+        scatter("vector", 1)
+        evac("scalar", 3)
+        sigmoid_of_pa(3)
+        add_old(2)
+        add_old(3)
+        scatter("scalar", 2)
+        scatter("vector", 3)
+        gain_round("scalar", 0)
+        gain_round("vector", 1)
+        gain_round("scalar", 2)
+        gain_round("vector", 3)
+
+        z_words = tile("z_words", [P, S], U32)
+        z_scales = tile("z_scales", [P, S], U8)
+        for u in range(2):
+            cols = slice(HALF * u, HALF * (u + 1))
+            z_grouped = tile("z_grouped%d" % u, [P, HALF, PACK], BF16)
+            woven = z_grouped[:].rearrange("p (c i) t -> p c t i", i=4)
+            rows = z_rows[:, :, cols].rearrange("p t (c i) -> p c t i", i=4)
+            nc.vector.tensor_copy(out=woven, in_=rows)
+            nc.vector.quantize_mx(out=z_words[:, cols].bitcast(FP8X4), scales=z_scales[:, cols], in_=z_grouped[:].rearrange("p c t -> p (c t)"))
+            for t in range(PACK):
+                product(h_bank[t][:, cols], w2w, w2s, t, z_words[:, cols], z_scales[:, cols], False, u == 1)
+
+        ex = [tile("ex%d" % t, [P, S], F32) for t in range(PACK)]
+        inv_ex = tile("inv_ex", [P, PACK, S], F32)
+        for t in range(PACK):
+            nc.scalar.activation(ex[t][:], h_bank[t][:], ACT.Exp, scale=0.5)
+        for t in range(PACK):
+            nc.scalar.activation(inv_ex[:, t, :], h_bank[t][:], ACT.Exp, scale=-0.5)
+
+        out_rows = out_0.rearrange("(p t) c -> p t c", t=PACK)
+        out_words_hbm = out_1[0].rearrange("p n t -> p (n t)").bitcast(I32)
+        o_words = tile("o_words", [P, S], U32)
+        o_scales = tile("o_scales", [P, S], U8)
+        for first, width, engine, square_engine in CHUNKS:
+            cols = slice(first, first + width)
+            entries = slice(first // 16, (first + width) // 16)
+            ex3 = tile("ex3_%d" % first, [P, PACK, width], F32)
+            both = tile("both_%d" % first, [P, PACK, width], F32)
+            ratio = tile("ratio_%d" % first, [P, PACK, width], F32)
+            root = tile("root_%d" % first, [P, PACK, width], F32)
+            share = tile("share_%d" % first, [P, PACK, width], F32)
+            grouped = tile("grouped_%d" % first, [P, width, PACK], BF16)
+            for t in range(PACK):
+                gather(engine, ex3[:, t, :], ex[t][:], n3_t[:, entries])
+                nc.vector.tensor_tensor(both[:, t, :], ex[t][:].indirect(n4_t[:, entries]), ex3[:, t, :], ALU.add)
+            nc.vector.tensor_tensor(ratio[:], both[:], inv_ex[:, :, cols], ALU.mult)
+            nc.scalar.activation(root[:], ratio[:], ACT.Abs_reciprocal_sqrt, scale=0.5, bias=0.5)
+            if square_engine == "scalar":
+                nc.scalar.activation(share[:], root[:], ACT.Square)
+            else:
+                nc.vector.tensor_tensor(share[:], root[:], root[:], ALU.mult)
+            nc.sync.dma_start(out=out_rows[:, :, cols], in_=share[:])
+            nc.vector.tensor_copy(
+                out=grouped[:].rearrange("p (c i) t -> p c t i", i=4),
+                in_=share[:].rearrange("p t (c i) -> p c t i", i=4),
+            )
+            nc.vector.quantize_mx(out=o_words[:, cols].bitcast(FP8X4), scales=o_scales[:, cols], in_=grouped[:].rearrange("p c t -> p (c t)"))
+            nc.sync.dma_start(out=out_words_hbm[:, cols], in_=o_words[:, cols].bitcast(I32))
+        for q in range(4):
+            queue = nc.scalar if q % 2 else nc.sync
+            queue.dma_start(out=out_2[0][4 * q : 4 * q + 4, :].bitcast(I32), in_=o_scales[32 * q : 32 * q + 4, :].bitcast(I32))

@@ -41,12 +41,9 @@ def tile_picked_hmixktanhshare_none_po_kernel(
             nc.sync.dma_start(held[:], src)
             return held
 
-        def load_scale_rows(queue, dst, src):
-            queue.dma_start(out=dst.bitcast(I32), in_=src[0].bitcast(I32))
-
-        def move_scale_rows(queue, dst, src):
-            for r in range(1, 4):
-                queue.dma_start(out=dst[r:P:32, :].bitcast(I32), in_=src[8 * r : P : 32, :].bitcast(I32))
+        def spread_scale_rows(plane, rows):
+            for q in range(4):
+                nc.sync.dma_start(out=plane[32 * q : 32 * q + 4, :].bitcast(I32), in_=rows[32 * q : 32 * q + 32 : 8, :].bitcast(I32))
 
         def deal_words(name, raw):
             dealt = tile(name, [P, 2 * N], U8)
@@ -56,69 +53,72 @@ def tile_picked_hmixktanhshare_none_po_kernel(
             )
             return dealt
 
-        def deal_scales(name, raw, count):
+        def deal_scales(engine, name, raw, count):
             dealt = tile(name, [P, count * N], U8)
-            nc.vector.tensor_copy(
+            engine.tensor_copy(
                 out=dealt[:].rearrange("p (w t m) -> p w t m", w=count, t=PACK),
                 in_=raw[:].rearrange("p (w m t) -> p w t m", w=count, t=PACK),
             )
             return dealt
 
-        def pick_scales(name, offsets, queue):
-            picked = tile(name + "_picked", [P, S], U8)
+        def pick_scales(name, plane, offsets):
+            picked = tile(name, [P, S], U8)
             nc.vector.tensor_copy(picked[:], xs_table[:].indirect(offsets))
-            plane = tile(name, [P, S], U8)
-            nc.vector.tensor_copy(plane[:].bitcast(I32), picked[:].bitcast(I32))
-            move_scale_rows(queue, plane, picked)
-            return plane
+            spread_scale_rows(plane, picked)
 
         xs_table = tile("xs_table", [P, T], U8)
-        nc.gpsimd.memset(xs_table[:].bitcast(I32), 0)
+        nc.vector.memset(xs_table[:, 0 : T // 2].bitcast(I32), 0)
+        nc.gpsimd.memset(xs_table[:, T // 2 : T].bitcast(I32), 0)
         w1s_raw = tile("w1s_raw", [P, H], U8)
-        nc.vector.memset(w1s_raw[:].bitcast(I32), 0)
+        nc.gpsimd.memset(w1s_raw[:].bitcast(I32), 0)
+        xs_offs = tile("xs_offs", [P, S], U8)
+        nc.vector.memset(xs_offs[:].bitcast(I32), 0)
+        xs_two = tile("xs_two", [P, S], U8)
+        nc.vector.memset(xs_two[:].bitcast(I32), 0)
         w23s_raw = tile("w23s_raw", [P, 2 * N], U8)
         nc.vector.memset(w23s_raw[:].bitcast(I32), 0)
+        w23s = tile("w23s", [P, 2 * N], U8)
+        nc.vector.memset(w23s[:].bitcast(I32), 0)
         half_ds = [tile("half_ds%d" % t, [P, WINDOW], F32) for t in range(PACK)]
-        for t in range(PACK):
-            nc.vector.memset(half_ds[t][:, S:WINDOW], 0.0)
+        nc.vector.memset(half_ds[0][:, S:WINDOW], 0.0)
         minus_half = tile("minus_half", [P, W], F32)
         nc.vector.memset(minus_half[:], -0.5)
 
-        xw_table = tile("xw_table", [P, T], U32)
-        nc.scalar.dma_start(out=xw_table[:].bitcast(I32), in_=x_words[0].rearrange("p n t -> p (n t)").bitcast(I32))
         offs_t = load_list("offs_t", offs)
-        load_scale_rows(nc.sync, xs_table[0:P:8, :], x_scales)
+        nc.sync.dma_start(out=xs_table[0:P:8, :].bitcast(I32), in_=x_scales[0].bitcast(I32))
         two_t = load_list("two_t", two)
-        n2_t = load_list("n2_t", n2)
-        n1_t = load_list("n1_t", n1)
-        n3_t = load_list("n3_t", n3)
-        n4_t = load_list("n4_t", n4)
-
-        load_scale_rows(nc.gpsimd, w1s_raw[0:P:8, :], w1_scales)
+        xw_table = tile("xw_table", [P, T], U32)
+        nc.sync.dma_start(out=xw_table[:].bitcast(I32), in_=x_words[0].rearrange("p n t -> p (n t)").bitcast(I32))
         w1w_raw = tile("w1w_raw", [P, 2 * H], U8)
         nc.gpsimd.dma_start(out=w1w_raw[:].bitcast(I32), in_=w1_words[0].bitcast(I32))
+        for q in range(4):
+            nc.scalar.dma_start(out=w1s_raw[32 * q : 32 * q + 4, :].bitcast(I32), in_=w1_scales[0][4 * q : 4 * q + 4, :].bitcast(I32))
         w3w_raw = tile("w3w_raw", [P, 2 * N], U8)
         nc.gpsimd.dma_start(out=w3w_raw[:].bitcast(I32), in_=w3_words[0].bitcast(I32))
         w2w_raw = tile("w2w_raw", [P, 2 * N], U8)
         nc.gpsimd.dma_start(out=w2w_raw[:].bitcast(I32), in_=w2_words[0].bitcast(I32))
-        load_scale_rows(nc.gpsimd, w23s_raw[0:P:8, 0:N], w2_scales)
-        load_scale_rows(nc.gpsimd, w23s_raw[0:P:8, N : 2 * N], w3_scales)
+        for t in range(1, PACK):
+            nc.gpsimd.memset(half_ds[t][:, S:WINDOW], 0.0)
         gain = tile("gain", [P, PACK], F32)
         nc.gpsimd.dma_start(out=gain[:], in_=gn.rearrange("(p t) o -> p (t o)", t=PACK))
 
-        xs_offs = pick_scales("xs_offs", offs_t[:], nc.scalar)
-        w1s = deal_scales("w1s", w1s_raw, 1)
-        move_scale_rows(nc.sync, w1s, w1s)
+        pick_scales("offs_picked", xs_offs, offs_t[:])
+        w1s = deal_scales(nc.vector, "w1s", w1s_raw, 1)
         w1w = deal_words("w1w", w1w_raw)
         xw_offs = tile("xw_offs", [P, S], U32)
         nc.vector.tensor_copy(xw_offs[:], xw_table[:].indirect(offs_t[:]))
-        xs_two = pick_scales("xs_two", two_t[:], nc.sync)
+        n2_t = load_list("n2_t", n2)
+        nc.sync.dma_start(out=w23s_raw[0:P:8, N : 2 * N].bitcast(I32), in_=w3_scales[0].bitcast(I32))
+        nc.sync.dma_start(out=w23s_raw[0:P:8, 0:N].bitcast(I32), in_=w2_scales[0].bitcast(I32))
+        n1_t = load_list("n1_t", n1)
         xw_two = tile("xw_two", [P, S], U32)
         nc.vector.tensor_copy(xw_two[:], xw_table[:].indirect(two_t[:]))
+        pick_scales("two_picked", xs_two, two_t[:])
+        spread_scale_rows(w23s, deal_scales(nc.gpsimd, "w23s_dealt", w23s_raw, 2))
+        n3_t = load_list("n3_t", n3)
+        n4_t = load_list("n4_t", n4)
         w3w = deal_words("w3w", w3w_raw)
         w2w = deal_words("w2w", w2w_raw)
-        w23s = deal_scales("w23s", w23s_raw, 2)
-        move_scale_rows(nc.sync, w23s, w23s)
         w2s = w23s[:, 0:N]
         w3s = w23s[:, N : 2 * N]
 
@@ -145,7 +145,7 @@ def tile_picked_hmixktanhshare_none_po_kernel(
         summed = [tile("summed%d" % t, [P, W], F32) for t in range(PACK)]
         z_rows = tile("z_rows", [P, PACK, S], BF16)
         gain2 = tile("gain2", [P, PACK], F32)
-        nc.vector.tensor_scalar(gain2[:], gain[:], 2.0, None, ALU.mult)
+        nc.gpsimd.tensor_scalar(gain2[:], gain[:], 2.0, None, ALU.mult)
 
         def evac(engine, t):
             if engine == "vector":
@@ -165,6 +165,12 @@ def tile_picked_hmixktanhshare_none_po_kernel(
         def add_old(t):
             nc.vector.tensor_tensor(summed[t][:], half_ds[t][:].indirect(n1_t[:]), sig[t][:], ALU.add)
 
+        def old_less_half(t):
+            nc.scalar.activation(summed[t][:], half_ds[t][:].indirect(n1_t[:]), ACT.Copy, bias=-0.5)
+
+        def scatter_sum(t):
+            nc.vector.tensor_tensor(half_ds[t][:].indirect(n1_t[:]), summed[t][:], sig[t][:], ALU.add)
+
         def scatter(engine, t):
             if engine == "vector":
                 nc.vector.tensor_tensor(half_ds[t][:].indirect(n1_t[:]), summed[t][:], minus_half[:], ALU.add)
@@ -181,20 +187,20 @@ def tile_picked_hmixktanhshare_none_po_kernel(
         sigmoid_of_pa(0)
         evac("vector", 1)
         sigmoid_of_pa(1)
-        add_old(0)
         evac("vector", 2)
+        add_old(0)
+        evac("vector", 3)
         sigmoid_of_pa(2)
-        add_old(1)
-        scatter("scalar", 0)
-        scatter("vector", 1)
-        evac("scalar", 3)
         sigmoid_of_pa(3)
+        old_less_half(3)
+        add_old(1)
+        scatter("vector", 0)
+        scatter("scalar", 1)
         add_old(2)
-        add_old(3)
         scatter("scalar", 2)
-        scatter("vector", 3)
-        gain_round("scalar", 0)
-        gain_round("vector", 1)
+        scatter_sum(3)
+        gain_round("vector", 0)
+        gain_round("scalar", 1)
         gain_round("scalar", 2)
         gain_round("vector", 3)
 
@@ -205,7 +211,11 @@ def tile_picked_hmixktanhshare_none_po_kernel(
             z_grouped = tile("z_grouped%d" % u, [P, HALF, PACK], BF16)
             woven = z_grouped[:].rearrange("p (c i) t -> p c t i", i=4)
             rows = z_rows[:, :, cols].rearrange("p t (c i) -> p c t i", i=4)
-            nc.vector.tensor_copy(out=woven, in_=rows)
+            if u == 0:
+                nc.vector.tensor_copy(out=woven, in_=rows)
+            else:
+                nc.vector.tensor_copy(out=woven[:, 0:32], in_=rows[:, 0:32])
+                nc.scalar.copy(out=woven[:, 32:64], in_=rows[:, 32:64])
             nc.vector.quantize_mx(out=z_words[:, cols].bitcast(FP8X4), scales=z_scales[:, cols], in_=z_grouped[:].rearrange("p c t -> p (c t)"))
             for t in range(PACK):
                 product(h_bank[t][:, cols], w2w, w2s, t, z_words[:, cols], z_scales[:, cols], False, u == 1)

@@ -20,7 +20,7 @@ P = 128
 PACK = 4
 WINDOW = 2 * W
 HALF = S // 2
-CHUNKS = ((0, 256, "vector", "scalar"), (256, 128, "scalar", "vector"), (384, 128, "scalar", "scalar"))
+QUARTER = S // 4
 
 
 def tile_picked_hmixktanhshare_none_po_kernel(
@@ -41,9 +41,9 @@ def tile_picked_hmixktanhshare_none_po_kernel(
             nc.sync.dma_start(held[:], src)
             return held
 
-        def spread_scale_rows(plane, rows):
+        def spread_scale_rows(plane, rows, first=0):
             for q in range(4):
-                nc.sync.dma_start(out=plane[32 * q : 32 * q + 4, :].bitcast(I32), in_=rows[32 * q : 32 * q + 32 : 8, :].bitcast(I32))
+                nc.sync.dma_start(out=plane[32 * q : 32 * q + 4, :].bitcast(I32), in_=rows[32 * q + first : 32 * q + 32 : 8, :].bitcast(I32))
 
         def deal_words(name, raw):
             dealt = tile(name, [P, 2 * N], U8)
@@ -53,11 +53,11 @@ def tile_picked_hmixktanhshare_none_po_kernel(
             )
             return dealt
 
-        def deal_scales(engine, name, raw, count):
-            dealt = tile(name, [P, count * N], U8)
-            engine.tensor_copy(
-                out=dealt[:].rearrange("p (w t m) -> p w t m", w=count, t=PACK),
-                in_=raw[:].rearrange("p (w m t) -> p w t m", w=count, t=PACK),
+        def deal_scales(name, raw):
+            dealt = tile(name, [P, N], U8)
+            nc.vector.tensor_copy(
+                out=dealt[:].rearrange("p (t m) -> p t m", t=PACK),
+                in_=raw[:].rearrange("p (m t) -> p t m", t=PACK),
             )
             return dealt
 
@@ -75,7 +75,7 @@ def tile_picked_hmixktanhshare_none_po_kernel(
         nc.vector.memset(xs_offs[:].bitcast(I32), 0)
         xs_two = tile("xs_two", [P, S], U8)
         nc.vector.memset(xs_two[:].bitcast(I32), 0)
-        w23s_raw = tile("w23s_raw", [P, 2 * N], U8)
+        w23s_raw = tile("w23s_raw", [P, N], U8)
         nc.vector.memset(w23s_raw[:].bitcast(I32), 0)
         w23s = tile("w23s", [P, 2 * N], U8)
         nc.vector.memset(w23s[:].bitcast(I32), 0)
@@ -103,18 +103,20 @@ def tile_picked_hmixktanhshare_none_po_kernel(
         nc.gpsimd.dma_start(out=gain[:], in_=gn.rearrange("(p t) o -> p (t o)", t=PACK))
 
         pick_scales("offs_picked", xs_offs, offs_t[:])
-        w1s = deal_scales(nc.vector, "w1s", w1s_raw, 1)
+        w1s = deal_scales("w1s", w1s_raw)
         w1w = deal_words("w1w", w1w_raw)
         xw_offs = tile("xw_offs", [P, S], U32)
         nc.vector.tensor_copy(xw_offs[:], xw_table[:].indirect(offs_t[:]))
         n2_t = load_list("n2_t", n2)
-        nc.sync.dma_start(out=w23s_raw[0:P:8, N : 2 * N].bitcast(I32), in_=w3_scales[0].bitcast(I32))
-        nc.sync.dma_start(out=w23s_raw[0:P:8, 0:N].bitcast(I32), in_=w2_scales[0].bitcast(I32))
+        nc.sync.dma_start(out=w23s_raw[0:P:8, :].bitcast(I32), in_=w3_scales[0].bitcast(I32))
+        nc.sync.dma_start(out=w23s_raw[4:P:8, :].bitcast(I32), in_=w2_scales[0].bitcast(I32))
         n1_t = load_list("n1_t", n1)
         xw_two = tile("xw_two", [P, S], U32)
         nc.vector.tensor_copy(xw_two[:], xw_table[:].indirect(two_t[:]))
         pick_scales("two_picked", xs_two, two_t[:])
-        spread_scale_rows(w23s, deal_scales(nc.gpsimd, "w23s_dealt", w23s_raw, 2))
+        w23s_dealt = deal_scales("w23s_dealt", w23s_raw)
+        spread_scale_rows(w23s[:, N : 2 * N], w23s_dealt, 0)
+        spread_scale_rows(w23s[:, 0:N], w23s_dealt, 4)
         n3_t = load_list("n3_t", n3)
         n4_t = load_list("n4_t", n4)
         w3w = deal_words("w3w", w3w_raw)
@@ -217,7 +219,9 @@ def tile_picked_hmixktanhshare_none_po_kernel(
                 nc.vector.tensor_copy(out=woven[:, 0:32], in_=rows[:, 0:32])
                 nc.scalar.copy(out=woven[:, 32:64], in_=rows[:, 32:64])
             nc.vector.quantize_mx(out=z_words[:, cols].bitcast(FP8X4), scales=z_scales[:, cols], in_=z_grouped[:].rearrange("p c t -> p (c t)"))
-            for t in range(PACK):
+        for t in range(PACK):
+            for u in range(2):
+                cols = slice(HALF * u, HALF * (u + 1))
                 product(h_bank[t][:, cols], w2w, w2s, t, z_words[:, cols], z_scales[:, cols], False, u == 1)
 
         ex = [tile("ex%d" % t, [P, S], F32) for t in range(PACK)]
@@ -231,24 +235,39 @@ def tile_picked_hmixktanhshare_none_po_kernel(
         out_words_hbm = out_1[0].rearrange("p n t -> p (n t)").bitcast(I32)
         o_words = tile("o_words", [P, S], U32)
         o_scales = tile("o_scales", [P, S], U8)
-        for first, width, engine, square_engine in CHUNKS:
-            cols = slice(first, first + width)
-            entries = slice(first // 16, (first + width) // 16)
-            ex3 = tile("ex3_%d" % first, [P, PACK, width], F32)
-            both = tile("both_%d" % first, [P, PACK, width], F32)
-            ratio = tile("ratio_%d" % first, [P, PACK, width], F32)
-            root = tile("root_%d" % first, [P, PACK, width], F32)
-            share = tile("share_%d" % first, [P, PACK, width], F32)
-            grouped = tile("grouped_%d" % first, [P, width, PACK], BF16)
-            for t in range(PACK):
-                gather(engine, ex3[:, t, :], ex[t][:], n3_t[:, entries])
-                nc.vector.tensor_tensor(both[:, t, :], ex[t][:].indirect(n4_t[:, entries]), ex3[:, t, :], ALU.add)
-            nc.vector.tensor_tensor(ratio[:], both[:], inv_ex[:, :, cols], ALU.mult)
+        ex3 = tile("ex_at_n3", [P, PACK, S], F32)
+        both = tile("both", [P, PACK, S], F32)
+
+        def fetch_n3(engine, t, u):
+            gather(engine, ex3[:, t, HALF * u : HALF * (u + 1)], ex[t][:], n3_t[:, 16 * u : 16 * (u + 1)])
+
+        def add_n4(t, u):
+            cols = slice(HALF * u, HALF * (u + 1))
+            nc.vector.tensor_tensor(both[:, t, cols], ex[t][:].indirect(n4_t[:, 16 * u : 16 * (u + 1)]), ex3[:, t, cols], ALU.add)
+
+        for t in (0, 1):
+            for u in range(2):
+                fetch_n3("vector", t, u)
+            for u in range(2):
+                add_n4(t, u)
+        for u in range(2):
+            for t in (2, 3):
+                fetch_n3("scalar", t, u)
+            for t in (2, 3):
+                add_n4(t, u)
+
+        for c in range(4):
+            cols = slice(QUARTER * c, QUARTER * (c + 1))
+            ratio = tile("ratio%d" % c, [P, PACK, QUARTER], F32)
+            root = tile("root%d" % c, [P, PACK, QUARTER], F32)
+            share = tile("share%d" % c, [P, PACK, QUARTER], F32)
+            grouped = tile("grouped%d" % c, [P, QUARTER, PACK], BF16)
+            nc.vector.tensor_tensor(ratio[:], both[:, :, cols], inv_ex[:, :, cols], ALU.mult)
             nc.scalar.activation(root[:], ratio[:], ACT.Abs_reciprocal_sqrt, scale=0.5, bias=0.5)
-            if square_engine == "scalar":
-                nc.scalar.activation(share[:], root[:], ACT.Square)
-            else:
+            if c == 1:
                 nc.vector.tensor_tensor(share[:], root[:], root[:], ALU.mult)
+            else:
+                nc.scalar.activation(share[:], root[:], ACT.Square)
             nc.sync.dma_start(out=out_rows[:, :, cols], in_=share[:])
             nc.vector.tensor_copy(
                 out=grouped[:].rearrange("p (c i) t -> p c t i", i=4),

from contextlib import ExitStack

import concourse.mybir as mybir

K, T, S, N, H, W = 512, 2048, 512, 512, 512, 384
FLOPS = 2 * S * (K * H + H * N + K * N)

F32 = mybir.dt.float32
BF16 = mybir.dt.bfloat16
I32 = mybir.dt.int32
U32 = mybir.dt.uint32
U16 = mybir.dt.uint16
U8 = mybir.dt.uint8
FP8X4 = mybir.dt.float8_e4m3fn_x4
FP4X4 = mybir.dt.float4_e2m1fn_x4
ACT = mybir.ActivationFunctionType
ALU = mybir.AluOpType

P = 128
PACK = 4
WINDOW = 2 * W
HALF = S // 2
QUARTER = S // 4


def tile_picked_hmixktanhshare_none_po_kernel(
    tc, x_words, x_scales, w1_words, w1_scales, gn, w2_words, w2_scales, w3_words, w3_scales,
    offs, n1, n2, two, n3, n4, out_0, out_1, out_2,
):
    nc = tc.nc
    with ExitStack() as ctx:
        lists = ctx.enter_context(tc.tile_pool(name="lists", bufs=1))
        sb = ctx.enter_context(tc.tile_pool(name="sb", bufs=1))
        psum = ctx.enter_context(tc.psum_pool(name="psum", bufs=1))

        def tile(name, shape, dtype):
            return sb.tile(shape, dtype, name=name, align_bytes=64)

        def load_list(name, src):
            held = lists.tile(list(src.shape), U16, name=name)
            nc.sync.dma_start(held[:], src)
            return held

        def spread_scale_rows(plane, rows, first=0):
            for q in range(4):
                nc.sync.dma_start(out=plane[32 * q : 32 * q + 4, :].bitcast(I32), in_=rows[32 * q + first : 32 * q + 32 : 8, :].bitcast(I32))

        def deal_words(name, raw):
            dealt = tile(name, [P, 2 * N], U8)
            nc.scalar.copy(
                out=dealt[:].bitcast(U16).rearrange("p (t m) -> p t m", t=PACK),
                in_=raw[:].bitcast(U16).rearrange("p (m t) -> p t m", t=PACK),
            )
            return dealt

        def deal_scales(name, raw):
            dealt = tile(name, [P, N], U8)
            nc.vector.tensor_copy(
                out=dealt[:].rearrange("p (t m) -> p t m", t=PACK),
                in_=raw[:].rearrange("p (m t) -> p t m", t=PACK),
            )
            return dealt

        def pick_scales(name, plane, offsets):
            picked = tile(name, [P, S], U8)
            nc.vector.tensor_copy(picked[:], xs_table[:].indirect(offsets))
            spread_scale_rows(plane, picked)

        xs_table = tile("xs_table", [P, T], U8)
        nc.vector.memset(xs_table[:, 0 : T // 2].bitcast(I32), 0)
        nc.gpsimd.memset(xs_table[:, T // 2 : T].bitcast(I32), 0)
        w1s_raw = tile("w1s_raw", [P, H], U8)
        nc.gpsimd.memset(w1s_raw[:].bitcast(I32), 0)
        xs_offs = tile("xs_offs", [P, S], U8)
        nc.vector.memset(xs_offs[:].bitcast(I32), 0)
        xs_two = tile("xs_two", [P, S], U8)
        nc.vector.memset(xs_two[:].bitcast(I32), 0)
        w23s_raw = tile("w23s_raw", [P, N], U8)
        nc.vector.memset(w23s_raw[:].bitcast(I32), 0)
        w23s = tile("w23s", [P, 2 * N], U8)
        nc.vector.memset(w23s[:].bitcast(I32), 0)
        half_ds = [tile("half_ds%d" % t, [P, WINDOW], F32) for t in range(PACK)]
        nc.vector.memset(half_ds[0][:, S:WINDOW], 0.0)
        minus_half = tile("minus_half", [P, W], F32)
        nc.vector.memset(minus_half[:], -0.5)

        offs_t = load_list("offs_t", offs)
        nc.sync.dma_start(out=xs_table[0:P:8, :].bitcast(I32), in_=x_scales[0].bitcast(I32))
        two_t = load_list("two_t", two)
        xw_table = tile("xw_table", [P, T], U32)
        nc.sync.dma_start(out=xw_table[:].bitcast(I32), in_=x_words[0].rearrange("p n t -> p (n t)").bitcast(I32))
        w1w_raw = tile("w1w_raw", [P, 2 * H], U8)
        nc.gpsimd.dma_start(out=w1w_raw[:].bitcast(I32), in_=w1_words[0].bitcast(I32))
        for q in range(4):
            nc.scalar.dma_start(out=w1s_raw[32 * q : 32 * q + 4, :].bitcast(I32), in_=w1_scales[0][4 * q : 4 * q + 4, :].bitcast(I32))
        w3w_raw = tile("w3w_raw", [P, 2 * N], U8)
        nc.gpsimd.dma_start(out=w3w_raw[:].bitcast(I32), in_=w3_words[0].bitcast(I32))
        w2w_raw = tile("w2w_raw", [P, 2 * N], U8)
        nc.gpsimd.dma_start(out=w2w_raw[:].bitcast(I32), in_=w2_words[0].bitcast(I32))
        for t in range(1, PACK):
            nc.gpsimd.memset(half_ds[t][:, S:WINDOW], 0.0)
        gain = tile("gain", [P, PACK], F32)
        nc.gpsimd.dma_start(out=gain[:], in_=gn.rearrange("(p t) o -> p (t o)", t=PACK))

        pick_scales("offs_picked", xs_offs, offs_t[:])
        w1s = deal_scales("w1s", w1s_raw)
        w1w = deal_words("w1w", w1w_raw)
        xw_offs = tile("xw_offs", [P, S], U32)
        nc.vector.tensor_copy(xw_offs[:], xw_table[:].indirect(offs_t[:]))
        n2_t = load_list("n2_t", n2)
        nc.sync.dma_start(out=w23s_raw[0:P:8, :].bitcast(I32), in_=w3_scales[0].bitcast(I32))
        nc.sync.dma_start(out=w23s_raw[4:P:8, :].bitcast(I32), in_=w2_scales[0].bitcast(I32))
        n1_t = load_list("n1_t", n1)
        xw_two = tile("xw_two", [P, S], U32)
        nc.vector.tensor_copy(xw_two[:], xw_table[:].indirect(two_t[:]))
        pick_scales("two_picked", xs_two, two_t[:])
        w23s_dealt = deal_scales("w23s_dealt", w23s_raw)
        spread_scale_rows(w23s[:, N : 2 * N], w23s_dealt, 0)
        spread_scale_rows(w23s[:, 0:N], w23s_dealt, 4)
        n3_t = load_list("n3_t", n3)
        n4_t = load_list("n4_t", n4)
        w3w = deal_words("w3w", w3w_raw)
        w2w = deal_words("w2w", w2w_raw)
        w2s = w23s[:, 0:N]
        w3s = w23s[:, N : 2 * N]

        def product(bank, words, scales, t, rhs, rhs_scale, start, stop):
            nc.tensor.matmul_mx(
                out=bank,
                lhsT=words[:, 2 * P * t : 2 * P * (t + 1)].bitcast(FP4X4),
                lhsT_scale=scales[:, P * t : P * (t + 1)],
                rhs=rhs.bitcast(FP8X4),
                rhs_scale=rhs_scale,
                start=start,
                stop=stop,
            )

        y_bank = [psum.tile([P, S], F32, name="y_bank%d" % t) for t in range(PACK)]
        h_bank = [psum.tile([P, S], F32, name="h_bank%d" % t) for t in range(PACK)]
        for t in range(PACK):
            product(y_bank[t][:], w1w, w1s, t, xw_offs[:], xs_offs[:], True, True)

        for t in range(PACK):
            product(h_bank[t][:], w3w, w3s, t, xw_two[:], xs_two[:], True, False)

        sig = [tile("sig%d" % t, [P, W], F32) for t in range(PACK)]
        summed = [tile("summed%d" % t, [P, W], F32) for t in range(PACK)]
        z_rows = tile("z_rows", [P, PACK, S], BF16)
        gain2 = tile("gain2", [P, PACK], F32)
        nc.gpsimd.tensor_scalar(gain2[:], gain[:], 2.0, None, ALU.mult)

        def evac(engine, t):
            if engine == "vector":
                nc.vector.tensor_scalar(half_ds[t][:, 0:S], y_bank[t][:], 0.5, None, ALU.mult)
            else:
                nc.scalar.activation(half_ds[t][:, 0:S], y_bank[t][:], ACT.Copy, scale=0.5)

        def gather(engine, dst, window, offsets):
            if engine == "vector":
                nc.vector.tensor_copy(dst, window.indirect(offsets))
            else:
                nc.scalar.activation(dst, window.indirect(offsets), ACT.Copy)

        def sigmoid_of_pa(t):
            nc.scalar.activation(sig[t][:], half_ds[t][:].indirect(n2_t[:]), ACT.Sigmoid, scale=-4.0)

        def add_old(t):
            nc.vector.tensor_tensor(summed[t][:], half_ds[t][:].indirect(n1_t[:]), sig[t][:], ALU.add)

        def old_less_half(t):
            nc.scalar.activation(summed[t][:], half_ds[t][:].indirect(n1_t[:]), ACT.Copy, bias=-0.5)

        def scatter_sum(t):
            nc.vector.tensor_tensor(half_ds[t][:].indirect(n1_t[:]), summed[t][:], sig[t][:], ALU.add)

        def scatter(engine, t):
            if engine == "vector":
                nc.vector.tensor_tensor(half_ds[t][:].indirect(n1_t[:]), summed[t][:], minus_half[:], ALU.add)
            else:
                nc.scalar.activation(half_ds[t][:].indirect(n1_t[:]), summed[t][:], ACT.Copy, bias=-0.5)

        def gain_round(engine, t):
            if engine == "vector":
                nc.vector.tensor_scalar(z_rows[:, t, :], half_ds[t][:, 0:S], gain2[:, t : t + 1], None, ALU.mult)
            else:
                nc.scalar.activation(z_rows[:, t, :], half_ds[t][:, 0:S], ACT.Copy, scale=gain2[:, t : t + 1])

        evac("vector", 0)
        sigmoid_of_pa(0)
        evac("vector", 1)
        sigmoid_of_pa(1)
        evac("vector", 2)
        add_old(0)
        evac("vector", 3)
        sigmoid_of_pa(2)
        sigmoid_of_pa(3)
        old_less_half(3)
        add_old(1)
        scatter("vector", 0)
        scatter("scalar", 1)
        add_old(2)
        scatter("scalar", 2)
        scatter_sum(3)
        gain_round("vector", 0)
        gain_round("scalar", 1)
        gain_round("scalar", 2)
        gain_round("vector", 3)

        z_words = tile("z_words", [P, S], U32)
        z_scales = tile("z_scales", [P, S], U8)
        for u in range(2):
            cols = slice(HALF * u, HALF * (u + 1))
            z_grouped = tile("z_grouped%d" % u, [P, HALF, PACK], BF16)
            woven = z_grouped[:].rearrange("p (c i) t -> p c t i", i=4)
            rows = z_rows[:, :, cols].rearrange("p t (c i) -> p c t i", i=4)
            if u == 0:
                nc.vector.tensor_copy(out=woven, in_=rows)
            else:
                nc.vector.tensor_copy(out=woven[:, 0:32], in_=rows[:, 0:32])
                nc.scalar.copy(out=woven[:, 32:64], in_=rows[:, 32:64])
            nc.vector.quantize_mx(out=z_words[:, cols].bitcast(FP8X4), scales=z_scales[:, cols], in_=z_grouped[:].rearrange("p c t -> p (c t)"))
        for t in range(PACK):
            for u in range(2):
                cols = slice(HALF * u, HALF * (u + 1))
                product(h_bank[t][:, cols], w2w, w2s, t, z_words[:, cols], z_scales[:, cols], False, u == 1)

        ex = [tile("ex%d" % t, [P, S], F32) for t in range(PACK)]
        inv_ex = tile("inv_ex", [P, PACK, S], F32)
        for t in range(PACK):
            nc.scalar.activation(ex[t][:], h_bank[t][:], ACT.Exp, scale=0.5)
        for t in range(PACK):
            nc.scalar.activation(inv_ex[:, t, :], h_bank[t][:], ACT.Exp, scale=-0.5)

        out_rows = out_0.rearrange("(p t) c -> p t c", t=PACK)
        out_words_hbm = out_1[0].rearrange("p n t -> p (n t)").bitcast(I32)
        o_words = tile("o_words", [P, S], U32)
        o_scales = tile("o_scales", [P, S], U8)
        ex3 = tile("ex_at_n3", [P, PACK, S], F32)
        both = tile("both", [P, PACK, S], F32)

        def fetch_n3(engine, t, u):
            gather(engine, ex3[:, t, HALF * u : HALF * (u + 1)], ex[t][:], n3_t[:, 16 * u : 16 * (u + 1)])

        def add_n4(t, u):
            cols = slice(HALF * u, HALF * (u + 1))
            nc.vector.tensor_tensor(both[:, t, cols], ex[t][:].indirect(n4_t[:, 16 * u : 16 * (u + 1)]), ex3[:, t, cols], ALU.add)

        for t in (0, 1):
            for u in range(2):
                fetch_n3("vector", t, u)
            for u in range(2):
                add_n4(t, u)
        for u in range(2):
            for t in (2, 3):
                fetch_n3("scalar", t, u)
            for t in (2, 3):
                add_n4(t, u)

        for c in range(4):
            cols = slice(QUARTER * c, QUARTER * (c + 1))
            ratio = tile("ratio%d" % c, [P, PACK, QUARTER], F32)
            root = tile("root%d" % c, [P, PACK, QUARTER], F32)
            share = tile("share%d" % c, [P, PACK, QUARTER], F32)
            grouped = tile("grouped%d" % c, [P, QUARTER, PACK], BF16)
            nc.vector.tensor_tensor(ratio[:], both[:, :, cols], inv_ex[:, :, cols], ALU.mult)
            nc.scalar.activation(root[:], ratio[:], ACT.Abs_reciprocal_sqrt, scale=0.5, bias=0.5)
            if c == 1:
                nc.vector.tensor_tensor(share[:], root[:], root[:], ALU.mult)
            else:
                nc.scalar.activation(share[:], root[:], ACT.Square)
            nc.sync.dma_start(out=out_rows[:, :, cols], in_=share[:])
            nc.vector.tensor_copy(
                out=grouped[:].rearrange("p (c i) t -> p c t i", i=4),
                in_=share[:].rearrange("p t (c i) -> p c t i", i=4),
            )
            nc.vector.quantize_mx(out=o_words[:, cols].bitcast(FP8X4), scales=o_scales[:, cols], in_=grouped[:].rearrange("p c t -> p (c t)"))
            nc.sync.dma_start(out=out_words_hbm[:, cols], in_=o_words[:, cols].bitcast(I32))
        for q in range(4):
            queue = nc.scalar if q % 2 else nc.sync
            queue.dma_start(out=out_2[0][4 * q : 4 * q + 4, :].bitcast(I32), in_=o_scales[32 * q : 32 * q + 4, :].bitcast(I32))
